import numpy as np
import ml_dtypes


def mxq(x, axis, fmt="e4m3"):
    dtype, down = {"e4m3": (ml_dtypes.float8_e4m3fn, 7), "e5m2": (ml_dtypes.float8_e5m2, 14)}[fmt]
    v = np.moveaxis(np.asarray(x, np.float32).astype(ml_dtypes.bfloat16).astype(np.float64), axis, -1)
    blocks = v.reshape(v.shape[:-1] + (-1, 32))
    amax = np.abs(blocks).max(-1, keepdims=True)
    byte = np.maximum(np.where(amax > 0, np.frexp(amax)[1] - 1 + 127, 0) - down, 1)
    scale = np.exp2(byte - 127.0)
    codes = (blocks / scale).astype(np.float32).astype(dtype).astype(np.float64)
    return np.moveaxis((codes * scale).reshape(v.shape), -1, axis)


WIDE = False


def mx_kscale(k):
    if not WIDE:
        return np.ones(k)
    levels = np.array([30, -30])
    if k % 512:
        return np.exp2(np.random.permutation(np.resize(levels, k // 32))).repeat(32)
    a = np.empty((k // 512, 16))
    for p in range(k // 512):
        a[p, :8] = np.random.permutation(np.resize(levels, 8))
        for g in range(8):
            far = levels[np.abs(levels - a[p, g]) >= 10]
            a[p, g + 8] = far[np.random.randint(len(far))]
    return np.exp2(a.ravel()).repeat(32)


BF16 = ml_dtypes.bfloat16


def bf(x):
    return np.asarray(x, np.float32).astype(BF16)


def f64(x):
    return np.asarray(x).astype(np.float64)


M, K, N, P, R = 1024, 1024, 1024, 1024, 512

OWN, OTHER = 0.8, 0.4


def silu(v):
    return 0.5 * v * (1.0 + np.tanh(0.5 * v))


def setup_inputs():
    s = mx_kscale(K)
    t = mx_kscale(N)
    v = mx_kscale(N)
    return {"x": bf(np.random.standard_normal((M, K)) * s),
            "w_a": bf(np.random.standard_normal((K, N)) / np.sqrt(K) / s[:, None]),
            "w_b": bf(np.random.standard_normal((K, N)) / np.sqrt(K) / s[:, None]),
            "b_a": bf(0.3 * np.random.standard_normal(N)),
            "b_b": bf(0.3 * np.random.standard_normal(N)),
            "st_aa": bf((OWN + 0.1 * np.random.standard_normal(N)) * t),
            "st_ab": bf((OTHER + 0.1 * np.random.standard_normal(N)) * t),
            "st_ba": bf((OTHER + 0.1 * np.random.standard_normal(N)) * v),
            "st_bb": bf((OWN + 0.1 * np.random.standard_normal(N)) * v),
            "u_a": bf(1.5 * np.random.standard_normal((N, P)) / np.sqrt(N) / t[:, None]),
            "u_b": bf(1.5 * np.random.standard_normal((N, R)) / np.sqrt(N) / v[:, None]),
            "c_a": bf(0.3 * np.random.standard_normal(P)),
            "c_b": bf(0.3 * np.random.standard_normal(R))}


def reference(x, w_a, w_b, b_a, b_b, st_aa, st_ab, st_ba, st_bb, u_a, u_b, c_a, c_b):
    xq = mxq(f64(x), 1, "e4m3")
    h_a = silu((xq @ mxq(f64(w_a), 0, "e4m3")) + f64(b_a))
    h_b = silu((xq @ mxq(f64(w_b), 0, "e4m3")) + f64(b_b))
    z_a = f64(st_aa) * h_a + f64(st_ab) * h_b
    z_b = f64(st_ba) * h_a + f64(st_bb) * h_b
    y_a = (mxq(z_a, 1, "e5m2") @ mxq(f64(u_a), 0, "e4m3")) + f64(c_a)
    y_b = np.tanh((mxq(z_b, 1, "e5m2") @ mxq(f64(u_b), 0, "e4m3")) + f64(c_b))
    return y_a, y_b

@@ -1,0 +1,364 @@
+from contextlib import ExitStack
+
+import concourse.mybir as mybir
+from concourse.masks import make_identity
+
+M, K, N, PA, RB = 1024, 1024, 1024, 1024, 512
+FLOPS = 2 * M * K * 2 * N + 2 * M * N * (PA + RB)
+
+F32 = mybir.dt.float32
+BF16 = mybir.dt.bfloat16
+U32 = mybir.dt.uint32
+U8 = mybir.dt.uint8
+E4M3 = mybir.dt.float8_e4m3fn_x4
+E5M2 = mybir.dt.float8_e5m2_x4
+ACT = mybir.ActivationFunctionType
+ALU = mybir.AluOpType
+
+P = 128
+PACK = 4
+KP = P * PACK
+BANK = 512
+CHUNKS = ((0, 256), (256, 512), (768, 128), (896, 128))
+
+
+def tile_cross_stitch_task_heads_f3_kernel(
+    tc, x, w_a, w_b, b_a, b_b, st_aa, st_ab, st_ba, st_bb, u_a, u_b, c_a, c_b, out_0, out_1
+):
+    nc = tc.nc
+    with ExitStack() as ctx:
+        keep = ctx.enter_context(tc.tile_pool(name="keep", bufs=1))
+        work = ctx.enter_context(tc.tile_pool(name="work", bufs=2))
+        psum = ctx.enter_context(tc.psum_pool(name="psum", bufs=8))
+        ctx.enter_context(tc.manual_schedule())
+
+        ident32 = keep.tile([P, P], F32, name="ident32")
+        make_identity(nc, ident32[:])
+        ident16 = keep.tile([P, P], BF16, name="ident16")
+        make_identity(nc, ident16[:])
+
+        vec_rows = keep.tile([P, KP], BF16, name="vec_rows")
+        nc.vector.memset(vec_rows[:], 0.0)
+        for i, v in enumerate((b_a, b_b, st_aa, st_ab, st_ba, st_bb)):
+            nc.scalar.dma_start(out=vec_rows[2 * i : 2 * i + 2, :], in_=v.rearrange("(g c) -> g c", g=2))
+        vec = keep.tile([P, PACK, 12], F32, name="vec")
+
+        def spread_vectors():
+            bank = psum.tile([P, PACK, P], BF16, name="bank")
+            for t in range(PACK):
+                nc.tensor.transpose(bank[:, t, :], vec_rows[:, t::PACK], ident16[:])
+            nc.scalar.copy(out=vec[:], in_=bank[:, :, 0:12])
+
+        raw = {}
+
+        def load_block(key, src, kp, half):
+            t = keep.tile([P, PACK, BANK], BF16, name="raw_%s%d%d" % key)
+            rows = src[kp * KP : (kp + 1) * KP, half * BANK : (half + 1) * BANK]
+            nc.sync.dma_start(out=t[:], in_=rows.rearrange("(p j) c -> p j c", j=PACK))
+            raw[key] = t
+
+        def load_x(a):
+            t = keep.tile([P, K], BF16, name="x_raw%d" % a)
+            nc.sync.dma_start(out=t[:], in_=x[a * P : (a + 1) * P, :])
+            raw[("x", a)] = t
+
+        srcs = {"wa": w_a, "wb": w_b, "ua": u_a, "ub": u_b}
+        for key in LOADS:
+            if key[0] == "x":
+                load_x(key[1])
+            else:
+                load_block(key, srcs[key[0]], key[1], key[2])
+        ca_all = keep.tile([P, PA], BF16, name="ca_all")
+        nc.sync.dma_start(out=ca_all[:], in_=c_a.partition_broadcast(P))
+        cb_all = keep.tile([P, RB], BF16, name="cb_all")
+        nc.sync.dma_start(out=cb_all[:], in_=c_b.partition_broadcast(P))
+
+        grouped = {}
+        codes = {}
+        scales = {}
+
+        def group_direct(key, src, width, permute, shared):
+            t = work.tile([P, PACK * width], BF16, name="grouped", bufs=4, align_bytes=64)
+            if permute:
+                dst = t[:].rearrange("p (t c i j) -> p c j i t", t=PACK, i=2, j=PACK)
+                rows = src[:].rearrange("p j (c i t) -> p c j i t", i=2, t=PACK)
+                nc.vector.tensor_copy(out=dst[:, :, :, :, 0:shared], in_=rows[:, :, :, :, 0:shared])
+                if shared < PACK:
+                    nc.scalar.copy(out=dst[:, :, :, :, shared:], in_=rows[:, :, :, :, shared:])
+            else:
+                nc.vector.tensor_copy(
+                    out=t[:].rearrange("p (c i j) -> p c j i", i=4, j=PACK),
+                    in_=src[:].rearrange("p j (c i) -> p c j i", i=4),
+                )
+            grouped[key] = t
+
+        staged = {}
+
+        def group_tensor(key, src, width, permute):
+            staged[key] = []
+            span = min(width, 256)
+            for h in range(width // span):
+                bank = psum.tile([P, PACK * span], BF16, name="bank")
+                cols = src[:, :, h * span : (h + 1) * span]
+                for jh in range(2):
+                    if permute:
+                        o = bank[:].rearrange("p (t m j) -> p m t j", t=PACK, j=PACK)[:, :, :, 2 * jh : 2 * jh + 2]
+                        r = cols[:, 2 * jh : 2 * jh + 2, :].rearrange("p j (m t) -> p m t j", t=PACK)
+                    else:
+                        o = bank[:].rearrange("p (c j) -> p c j", j=PACK)[:, :, 2 * jh : 2 * jh + 2]
+                        r = cols[:, 2 * jh : 2 * jh + 2, :].rearrange("p j c -> p c j")
+                    nc.tensor.matmul(out=o, lhsT=ident16[:], rhs=r, start=True, stop=True)
+                staged[key].append(bank)
+
+        def unstage(key, width, permute):
+            t = work.tile([P, PACK * width], BF16, name="grouped", bufs=4, align_bytes=64)
+            span = PACK * min(width, 256)
+            for h, bank in enumerate(staged.pop(key)):
+                if permute:
+                    nc.scalar.copy(
+                        out=t[:].rearrange("p (t e) -> p t e", t=PACK)[:, :, h * 256 : (h + 1) * 256],
+                        in_=bank[:].rearrange("p (t e) -> p t e", t=PACK),
+                    )
+                else:
+                    nc.scalar.copy(out=t[:, h * span : (h + 1) * span], in_=bank[:])
+            grouped[key] = t
+
+        def quantize_block(key):
+            c = keep.tile([P, BANK], U32, name="codes_%s%d%d" % key, align_bytes=64)
+            s = keep.tile([P, BANK], U8, name="scales_%s%d%d" % key, align_bytes=64)
+            nc.vector.quantize_mx(out=c[:].bitcast(E4M3), scales=s[:], in_=grouped.pop(key)[:])
+            codes[key], scales[key] = c, s
+
+        xt = {}
+
+        xbank = {}
+
+        def transpose_x(ci, a):
+            t0, width = CHUNKS[ci]
+            words = raw[("x", t0 // P + a)][:].bitcast(F32)
+            bank = psum.tile([P, 2, 2, P], F32, name="bank")
+            for kp in range(2):
+                for u in range(2):
+                    nc.tensor.transpose(bank[:, kp, u, :], words[:, 256 * kp + u : 256 * (kp + 1) : 2], ident32[:])
+            xbank[(ci, a)] = bank
+
+        def unstage_x(ci, a):
+            width = CHUNKS[ci][1]
+            if ci not in xt:
+                xt[ci] = work.tile([P, 2, width, 2], F32, name="xt%d" % width, bufs=1, align_bytes=64)
+            nc.scalar.copy(
+                out=xt[ci][:, :, a * P : (a + 1) * P, :], in_=xbank.pop((ci, a))[:].rearrange("p k u r -> p k r u")
+            )
+
+        def quantize_x(ci):
+            width = CHUNKS[ci][1]
+            c = keep.tile([P, 2 * width], U32, name="codes_x%d" % ci, align_bytes=64)
+            s = keep.tile([P, 2 * width], U8, name="scales_x%d" % ci, align_bytes=64)
+            nc.vector.quantize_mx(
+                out=c[:].bitcast(E4M3), scales=s[:], in_=xt[ci][:].rearrange("p k r u -> p (k r u)").bitcast(BF16)
+            )
+            codes[("x", ci)], scales[("x", ci)] = c, s
+
+        units = [(ci, g, t) for ci in range(len(CHUNKS)) for g in range(2) for t in range(PACK)]
+        pre = {}
+        hidden = {}
+        zrows = {}
+
+        def branch_matmul(unit, nm):
+            ci, g, t = unit
+            width = CHUNKS[ci][1]
+            bank = psum.tile([P, width], F32, name="bank")
+            for kp in range(2):
+                key = (nm, kp, g)
+                nc.tensor.matmul_mx(
+                    out=bank[:],
+                    lhsT=codes[key][:, t * P : (t + 1) * P].bitcast(E4M3),
+                    lhsT_scale=scales[key][:, t * P : (t + 1) * P],
+                    rhs=codes[("x", ci)][:, kp * width : (kp + 1) * width].bitcast(E4M3),
+                    rhs_scale=scales[("x", ci)][:, kp * width : (kp + 1) * width],
+                    start=(kp == 0),
+                    stop=(kp == 1),
+                )
+            pre[(unit, nm)] = bank
+
+        def column(i, unit):
+            j = 2 * i + unit[1]
+            return vec[:, unit[2], j : j + 1]
+
+        def activate(unit):
+            width = CHUNKS[unit[0]][1]
+            h_a = work.tile([P, width], F32, name="h_a", bufs=4)
+            h_b = work.tile([P, width], F32, name="h_b", bufs=4)
+            nc.scalar.activation(out=h_a[:], in_=pre.pop((unit, "wa"))[:], func=ACT.Silu, bias=column(0, unit))
+            nc.scalar.activation(out=h_b[:], in_=pre.pop((unit, "wb"))[:], func=ACT.Silu, bias=column(1, unit))
+            hidden[unit] = (h_a, h_b)
+
+        def cross_terms(unit):
+            width = CHUNKS[unit[0]][1]
+            h_a, h_b = hidden[unit]
+            cross_a = work.tile([P, width], F32, name="cross_a", bufs=3)
+            cross_b = work.tile([P, width], F32, name="cross_b", bufs=3)
+            if units.index(unit) in CROSS_B_V:
+                nc.vector.tensor_scalar(out=cross_b[:], in0=h_a[:], scalar1=column(4, unit), scalar2=None, op0=ALU.mult)
+            else:
+                nc.scalar.activation(out=cross_b[:], in_=h_a[:], func=ACT.Copy, scale=column(4, unit))
+            nc.scalar.activation(out=cross_a[:], in_=h_b[:], func=ACT.Copy, scale=column(3, unit))
+            hidden[unit] = (h_a, h_b, cross_a, cross_b)
+
+        def stitch(unit):
+            ci, g, t = unit
+            width = CHUNKS[ci][1]
+            h_a, h_b, cross_a, cross_b = hidden.pop(unit)
+            if t == 0:
+                zrows[("zb", ci, g)] = work.tile([P, PACK, width], BF16, name="zrows_b")
+                zrows[("za", ci, g)] = work.tile([P, PACK, width], BF16, name="zrows_a")
+            nc.vector.scalar_tensor_tensor(
+                out=zrows[("zb", ci, g)][:, t, :], in0=h_b[:], scalar=column(5, unit), in1=cross_b[:], op0=ALU.mult, op1=ALU.add
+            )
+            nc.vector.scalar_tensor_tensor(
+                out=zrows[("za", ci, g)][:, t, :], in0=h_a[:], scalar=column(2, unit), in1=cross_a[:], op0=ALU.mult, op1=ALU.add
+            )
+
+        def quantize_z(key):
+            width = CHUNKS[key[1]][1]
+            c = keep.tile([P, width], U32, name="codes_%s%d%d" % key, align_bytes=64)
+            s = keep.tile([P, width], U8, name="scales_%s%d%d" % key, align_bytes=64)
+            nc.vector.quantize_mx(out=c[:].bitcast(E5M2), scales=s[:], in_=grouped.pop(key)[:])
+            codes[key], scales[key] = c, s
+
+        heads = {}
+        y_rows = {}
+
+        def head_matmul(ci, a, nm, half):
+            bank = psum.tile([P, BANK], F32, name="bank")
+            for g in range(2):
+                zkey, ukey = ("z" + nm, ci, g), ("u" + nm, g, half)
+                nc.tensor.matmul_mx(
+                    out=bank[:],
+                    lhsT=codes[zkey][:, a * P : (a + 1) * P].bitcast(E5M2),
+                    lhsT_scale=scales[zkey][:, a * P : (a + 1) * P],
+                    rhs=codes[ukey][:].bitcast(E4M3),
+                    rhs_scale=scales[ukey][:],
+                    start=(g == 0),
+                    stop=(g == 1),
+                )
+            heads[(ci, a, nm, half)] = bank
+
+        def head_finish(ci, a, nm, half):
+            bank = heads.pop((ci, a, nm, half))
+            rows = slice(CHUNKS[ci][0] + a * P, CHUNKS[ci][0] + (a + 1) * P)
+            cols = slice(half * BANK, (half + 1) * BANK)
+            if nm == "a":
+                y = work.tile([P, BANK], F32, name="y_a", bufs=4)
+                nc.vector.tensor_tensor(out=y[:], in0=bank[:], in1=ca_all[:, cols], op=ALU.add)
+                nc.sync.dma_start(out=out_0[rows, cols], in_=y[:])
+            else:
+                y = work.tile([P, BANK], F32, name="y_b", bufs=2)
+                nc.vector.tensor_tensor(out=y[:], in0=bank[:], in1=cb_all[:], op=ALU.add)
+                y_rows[(ci, a, "b")] = y
+
+        def head_tanh(ci, a):
+            rows = slice(CHUNKS[ci][0] + a * P, CHUNKS[ci][0] + (a + 1) * P)
+            yt = work.tile([P, BANK], F32, name="y_tanh", bufs=2)
+            nc.scalar.activation(out=yt[:], in_=y_rows.pop((ci, a, "b"))[:], func=ACT.Tanh)
+            nc.sync.dma_start(out=out_1[rows, :], in_=yt[:])
+
+        def group(key, route):
+            src = zrows.pop(key) if key[0][0] == "z" else raw[key]
+            if route == "T":
+                group_tensor(key, src, width_of(key), key[0][0] == "w")
+            else:
+                group_direct(key, src, width_of(key), key[0][0] == "w", PACK if route == "V" else route)
+
+        def quant(key):
+            if key[0][0] == "z":
+                quantize_z(key)
+            else:
+                quantize_block(key)
+
+        def width_of(key):
+            return CHUNKS[key[1]][1] if key[0][0] == "z" else BANK
+
+        group(("wa", 0, 0), 3)
+        spread_vectors()
+        transpose_x(0, 0)
+        unstage_x(0, 0)
+        quant(("wa", 0, 0))
+        transpose_x(0, 1)
+        unstage_x(0, 1)
+        group(("wa", 1, 0), 3)
+        quantize_x(0)
+        quant(("wa", 1, 0))
+        branch_matmul(units[0], "wa")
+        group(("wb", 0, 0), 2)
+        quant(("wb", 0, 0))
+        group(("wb", 1, 0), 2)
+        quant(("wb", 1, 0))
+        branch_matmul(units[0], "wb")
+
+        steps = len(units) + 8
+        on_tensor = [[] for u in range(steps)]
+        on_scalar = [[] for u in range(steps)]
+        early = [[] for u in range(steps)]
+        late = [[] for u in range(steps)]
+
+        def plan_block(step, key, route):
+            if route == "T":
+                on_tensor[step].append(lambda: group(key, route))
+                on_scalar[step + 1].append(lambda: unstage(key, width_of(key), key[0][0] == "w"))
+                late[step + 2].append(lambda: quant(key))
+            else:
+                late[step].append(lambda: group(key, route))
+                early[step + 1].append(lambda: quant(key))
+
+        def plan_head(step, args):
+            on_tensor[step].append(lambda: head_matmul(*args))
+            late[step + 1].append(lambda: head_finish(*args))
+            if args[2] == "b":
+                on_scalar[step + 2].append(lambda: head_tanh(args[0], args[1]))
+
+        def plan_x(step, ci):
+            tiles = CHUNKS[ci][1] // P
+            for a in range(tiles):
+                on_tensor[step + a].append(lambda a=a: transpose_x(ci, a))
+                on_scalar[step + a + 1].append(lambda a=a: unstage_x(ci, a))
+            early[step + tiles + 1].append(lambda: quantize_x(ci))
+
+        for s, key, route in SCHED:
+            plan_block(s, key, route)
+        for ci in range(1, len(CHUNKS)):
+            plan_x(XSTEP[ci - 1], ci)
+        for ci in range(len(CHUNKS)):
+            jobs = [(ci, a, nm, half) for a in range(CHUNKS[ci][1] // P) for nm, half in (("b", 0), ("a", 0), ("a", 1))]
+            for n, args in enumerate(jobs):
+                plan_head(HEADSTEP[ci][n], args)
+
+        for i in range(steps):
+            if i < len(units):
+                activate(units[i])
+            if 1 <= i <= len(units):
+                cross_terms(units[i - 1])
+            for fn in on_scalar[i]:
+                fn()
+            for fn in early[i]:
+                fn()
+            if 2 <= i <= len(units) + 1:
+                stitch(units[i - 2])
+            for fn in late[i]:
+                fn()
+            if i + 1 < len(units):
+                branch_matmul(units[i + 1], "wa")
+                branch_matmul(units[i + 1], "wb")
+            for fn in on_tensor[i]:
+                fn()
+
+
+LOADS = (("wa", 0, 0), ("x", 0), ("x", 1), ("wa", 1, 0), ("wb", 0, 0), ("wb", 1, 0), ("wa", 0, 1), ("wa", 1, 1), ("wb", 0, 1), ("wb", 1, 1),
+    ("x", 2), ("x", 3), ("x", 4), ("x", 5), ("ub", 0, 0), ("ub", 1, 0), ("ua", 0, 0), ("ua", 1, 0), ("ua", 0, 1), ("ua", 1, 1), ("x", 6), ("x", 7))
+SCHED = (
+    (0, ("wa", 0, 1), 3), (0, ("wb", 0, 1), "T"), (1, ("wa", 1, 1), "V"), (2, ("wb", 1, 1), "V"),
+    (4, ("ub", 0, 0), "V"), (6, ("ub", 1, 0), "V"), (7, ("ua", 0, 0), "V"), (8, ("ua", 1, 0), "V"), (8, ("ua", 0, 1), "T"), (9, ("ua", 1, 1), "T"),
+) + tuple((4 * q + 5 + n, (nm, q // 2, q % 2), "T") for q in range(7) for n, nm in enumerate(("zb", "za"))) + ((33, ("zb", 3, 1), "V"), (33, ("za", 3, 1), "V"))
+XSTEP = (1, 12, 20)
+HEADSTEP = ((11, 12, 12, 13, 14, 14), (20, 20, 21, 22, 22, 23, 24, 24, 25, 26, 26, 27), (28, 29, 30), (34, 34, 34))
+CROSS_B_V = (10, 11, 13, 14)

@@ -19,7 +19,7 @@ P = 128
 PACK = 4
 KP = P * PACK
 BANK = 512
-CHUNKS = ((0, 256), (256, 512), (768, 128), (896, 128))
+CHUNKS = ((0, 512), (512, 256), (768, 256))
 
 
 def tile_cross_stitch_task_heads_f3_kernel(
@@ -29,7 +29,7 @@ def tile_cross_stitch_task_heads_f3_kernel(
     with ExitStack() as ctx:
         keep = ctx.enter_context(tc.tile_pool(name="keep", bufs=1))
         work = ctx.enter_context(tc.tile_pool(name="work", bufs=2))
-        psum = ctx.enter_context(tc.psum_pool(name="psum", bufs=8))
+        psum = ctx.enter_context(tc.psum_pool(name="psum", bufs=4))
         ctx.enter_context(tc.manual_schedule())
 
         ident32 = keep.tile([P, P], F32, name="ident32")
@@ -42,6 +42,8 @@ def tile_cross_stitch_task_heads_f3_kernel(
         for i, v in enumerate((b_a, b_b, st_aa, st_ab, st_ba, st_bb)):
             nc.scalar.dma_start(out=vec_rows[2 * i : 2 * i + 2, :], in_=v.rearrange("(g c) -> g c", g=2))
         vec = keep.tile([P, PACK, 12], F32, name="vec")
+        warm = keep.tile([P, 1], F32, name="warm")
+        nc.scalar.activation(out=warm[:], in_=ident32[:, 0:1], func=ACT.Silu)
 
         def spread_vectors():
             bank = psum.tile([P, PACK, P], BF16, name="bank")
@@ -78,49 +80,22 @@ def tile_cross_stitch_task_heads_f3_kernel(
         scales = {}
 
         def group_direct(key, src, width, permute, shared):
-            t = work.tile([P, PACK * width], BF16, name="grouped", bufs=4, align_bytes=64)
+            t = work.tile([P, PACK * width], BF16, name="grouped", bufs=5, align_bytes=64)
             if permute:
                 dst = t[:].rearrange("p (t c i j) -> p c j i t", t=PACK, i=2, j=PACK)
                 rows = src[:].rearrange("p j (c i t) -> p c j i t", i=2, t=PACK)
-                nc.vector.tensor_copy(out=dst[:, :, :, :, 0:shared], in_=rows[:, :, :, :, 0:shared])
+                if shared > 0:
+                    nc.vector.tensor_copy(out=dst[:, :, :, :, 0:shared], in_=rows[:, :, :, :, 0:shared])
                 if shared < PACK:
                     nc.scalar.copy(out=dst[:, :, :, :, shared:], in_=rows[:, :, :, :, shared:])
             else:
-                nc.vector.tensor_copy(
-                    out=t[:].rearrange("p (c i j) -> p c j i", i=4, j=PACK),
-                    in_=src[:].rearrange("p j (c i) -> p c j i", i=4),
-                )
-            grouped[key] = t
-
-        staged = {}
-
-        def group_tensor(key, src, width, permute):
-            staged[key] = []
-            span = min(width, 256)
-            for h in range(width // span):
-                bank = psum.tile([P, PACK * span], BF16, name="bank")
-                cols = src[:, :, h * span : (h + 1) * span]
-                for jh in range(2):
-                    if permute:
-                        o = bank[:].rearrange("p (t m j) -> p m t j", t=PACK, j=PACK)[:, :, :, 2 * jh : 2 * jh + 2]
-                        r = cols[:, 2 * jh : 2 * jh + 2, :].rearrange("p j (m t) -> p m t j", t=PACK)
-                    else:
-                        o = bank[:].rearrange("p (c j) -> p c j", j=PACK)[:, :, 2 * jh : 2 * jh + 2]
-                        r = cols[:, 2 * jh : 2 * jh + 2, :].rearrange("p j c -> p c j")
-                    nc.tensor.matmul(out=o, lhsT=ident16[:], rhs=r, start=True, stop=True)
-                staged[key].append(bank)
-
-        def unstage(key, width, permute):
-            t = work.tile([P, PACK * width], BF16, name="grouped", bufs=4, align_bytes=64)
-            span = PACK * min(width, 256)
-            for h, bank in enumerate(staged.pop(key)):
-                if permute:
-                    nc.scalar.copy(
-                        out=t[:].rearrange("p (t e) -> p t e", t=PACK)[:, :, h * 256 : (h + 1) * 256],
-                        in_=bank[:].rearrange("p (t e) -> p t e", t=PACK),
-                    )
-                else:
-                    nc.scalar.copy(out=t[:, h * span : (h + 1) * span], in_=bank[:])
+                dst = t[:].rearrange("p (c i j) -> p c j i", i=4, j=PACK)
+                rows = src[:].rearrange("p j (c i) -> p c j i", i=4)
+                cut = shared * width // 16
+                if cut > 0:
+                    nc.vector.tensor_copy(out=dst[:, 0:cut], in_=rows[:, 0:cut])
+                if shared < PACK:
+                    nc.scalar.copy(out=dst[:, cut:], in_=rows[:, cut:])
             grouped[key] = t
 
         def quantize_block(key):
@@ -159,7 +134,7 @@ def tile_cross_stitch_task_heads_f3_kernel(
             )
             codes[("x", ci)], scales[("x", ci)] = c, s
 
-        units = [(ci, g, t) for ci in range(len(CHUNKS)) for g in range(2) for t in range(PACK)]
+        units = [(ci, g, t) for ci, g in QUADS for t in range(PACK)]
         pre = {}
         hidden = {}
         zrows = {}
@@ -167,7 +142,7 @@ def tile_cross_stitch_task_heads_f3_kernel(
         def branch_matmul(unit, nm):
             ci, g, t = unit
             width = CHUNKS[ci][1]
-            bank = psum.tile([P, width], F32, name="bank")
+            bank = psum.tile([P, width], F32, name="pre")
             for kp in range(2):
                 key = (nm, kp, g)
                 nc.tensor.matmul_mx(
@@ -187,8 +162,8 @@ def tile_cross_stitch_task_heads_f3_kernel(
 
         def activate(unit):
             width = CHUNKS[unit[0]][1]
-            h_a = work.tile([P, width], F32, name="h_a", bufs=4)
-            h_b = work.tile([P, width], F32, name="h_b", bufs=4)
+            h_a = work.tile([P, width], F32, name="h_a", bufs=HB)
+            h_b = work.tile([P, width], F32, name="h_b", bufs=HB)
             nc.scalar.activation(out=h_a[:], in_=pre.pop((unit, "wa"))[:], func=ACT.Silu, bias=column(0, unit))
             nc.scalar.activation(out=h_b[:], in_=pre.pop((unit, "wb"))[:], func=ACT.Silu, bias=column(1, unit))
             hidden[unit] = (h_a, h_b)
@@ -196,8 +171,8 @@ def tile_cross_stitch_task_heads_f3_kernel(
         def cross_terms(unit):
             width = CHUNKS[unit[0]][1]
             h_a, h_b = hidden[unit]
-            cross_a = work.tile([P, width], F32, name="cross_a", bufs=3)
-            cross_b = work.tile([P, width], F32, name="cross_b", bufs=3)
+            cross_a = work.tile([P, width], F32, name="cross_a", bufs=HB - 1)
+            cross_b = work.tile([P, width], F32, name="cross_b", bufs=HB - 1)
             if units.index(unit) in CROSS_B_V:
                 nc.vector.tensor_scalar(out=cross_b[:], in0=h_a[:], scalar1=column(4, unit), scalar2=None, op0=ALU.mult)
             else:
@@ -253,7 +228,7 @@ def tile_cross_stitch_task_heads_f3_kernel(
                 nc.vector.tensor_tensor(out=y[:], in0=bank[:], in1=ca_all[:, cols], op=ALU.add)
                 nc.sync.dma_start(out=out_0[rows, cols], in_=y[:])
             else:
-                y = work.tile([P, BANK], F32, name="y_b", bufs=2)
+                y = work.tile([P, BANK], F32, name="y_b", bufs=3)
                 nc.vector.tensor_tensor(out=y[:], in0=bank[:], in1=cb_all[:], op=ALU.add)
                 y_rows[(ci, a, "b")] = y
 
@@ -265,9 +240,7 @@ def tile_cross_stitch_task_heads_f3_kernel(
 
         def group(key, route):
             src = zrows.pop(key) if key[0][0] == "z" else raw[key]
-            if route == "T":
-                group_tensor(key, src, width_of(key), key[0][0] == "w")
-            else:
+            if True:
                 group_direct(key, src, width_of(key), key[0][0] == "w", PACK if route == "V" else route)
 
         def quant(key):
@@ -281,14 +254,15 @@ def tile_cross_stitch_task_heads_f3_kernel(
 
         group(("wa", 0, 0), 3)
         spread_vectors()
-        transpose_x(0, 0)
-        unstage_x(0, 0)
-        quant(("wa", 0, 0))
-        transpose_x(0, 1)
-        unstage_x(0, 1)
-        group(("wa", 1, 0), 3)
-        quantize_x(0)
+        for a in range(CHUNKS[0][1] // P):
+            transpose_x(0, a)
+            unstage_x(0, a)
+            if a == 0:
+                quant(("wa", 0, 0))
+            if a == 1:
+                group(("wa", 1, 0), 3)
         quant(("wa", 1, 0))
+        quantize_x(0)
         branch_matmul(units[0], "wa")
         group(("wb", 0, 0), 2)
         quant(("wb", 0, 0))
@@ -296,40 +270,39 @@ def tile_cross_stitch_task_heads_f3_kernel(
         quant(("wb", 1, 0))
         branch_matmul(units[0], "wb")
 
-        steps = len(units) + 8
+        steps = len(units) + 12
         on_tensor = [[] for u in range(steps)]
         on_scalar = [[] for u in range(steps)]
         early = [[] for u in range(steps)]
         late = [[] for u in range(steps)]
 
         def plan_block(step, key, route):
-            if route == "T":
-                on_tensor[step].append(lambda: group(key, route))
-                on_scalar[step + 1].append(lambda: unstage(key, width_of(key), key[0][0] == "w"))
-                late[step + 2].append(lambda: quant(key))
+            if route == 0:
+                on_scalar[step + SLAG].append(lambda: group(key, route))
+                late[step + SLAG + QLAG].append(lambda: quant(key))
             else:
                 late[step].append(lambda: group(key, route))
-                early[step + 1].append(lambda: quant(key))
+                late[step + 1].append(lambda: quant(key))
 
         def plan_head(step, args):
             on_tensor[step].append(lambda: head_matmul(*args))
-            late[step + 1].append(lambda: head_finish(*args))
+            late[step + HLAG].append(lambda: head_finish(*args))
             if args[2] == "b":
-                on_scalar[step + 2].append(lambda: head_tanh(args[0], args[1]))
+                on_scalar[step + HLAG + TLAG].append(lambda: head_tanh(args[0], args[1]))
 
         def plan_x(step, ci):
             tiles = CHUNKS[ci][1] // P
             for a in range(tiles):
                 on_tensor[step + a].append(lambda a=a: transpose_x(ci, a))
                 on_scalar[step + a + 1].append(lambda a=a: unstage_x(ci, a))
-            early[step + tiles + 1].append(lambda: quantize_x(ci))
+            late[step + tiles + 1].append(lambda: quantize_x(ci))
 
         for s, key, route in SCHED:
             plan_block(s, key, route)
         for ci in range(1, len(CHUNKS)):
             plan_x(XSTEP[ci - 1], ci)
         for ci in range(len(CHUNKS)):
-            jobs = [(ci, a, nm, half) for a in range(CHUNKS[ci][1] // P) for nm, half in (("b", 0), ("a", 0), ("a", 1))]
+            jobs = [(ci, a + da, nm, half) for a in range(0, CHUNKS[ci][1] // P, 2) for da, nm, half in ((0, "b", 0), (1, "b", 0), (0, "a", 0), (0, "a", 1), (1, "a", 0), (1, "a", 1))]
             for n, args in enumerate(jobs):
                 plan_head(HEADSTEP[ci][n], args)
 
@@ -342,8 +315,8 @@ def tile_cross_stitch_task_heads_f3_kernel(
                 fn()
             for fn in early[i]:
                 fn()
-            if 2 <= i <= len(units) + 1:
-                stitch(units[i - 2])
+            if VLAG <= i < len(units) + VLAG:
+                stitch(units[i - VLAG])
             for fn in late[i]:
                 fn()
             if i + 1 < len(units):
@@ -353,12 +326,16 @@ def tile_cross_stitch_task_heads_f3_kernel(
                 fn()
 
 
-LOADS = (("wa", 0, 0), ("x", 0), ("x", 1), ("wa", 1, 0), ("wb", 0, 0), ("wb", 1, 0), ("wa", 0, 1), ("wa", 1, 1), ("wb", 0, 1), ("wb", 1, 1),
-    ("x", 2), ("x", 3), ("x", 4), ("x", 5), ("ub", 0, 0), ("ub", 1, 0), ("ua", 0, 0), ("ua", 1, 0), ("ua", 0, 1), ("ua", 1, 1), ("x", 6), ("x", 7))
-SCHED = (
-    (0, ("wa", 0, 1), 3), (0, ("wb", 0, 1), "T"), (1, ("wa", 1, 1), "V"), (2, ("wb", 1, 1), "V"),
-    (4, ("ub", 0, 0), "V"), (6, ("ub", 1, 0), "V"), (7, ("ua", 0, 0), "V"), (8, ("ua", 1, 0), "V"), (8, ("ua", 0, 1), "T"), (9, ("ua", 1, 1), "T"),
-) + tuple((4 * q + 5 + n, (nm, q // 2, q % 2), "T") for q in range(7) for n, nm in enumerate(("zb", "za"))) + ((33, ("zb", 3, 1), "V"), (33, ("za", 3, 1), "V"))
-XSTEP = (1, 12, 20)
-HEADSTEP = ((11, 12, 12, 13, 14, 14), (20, 20, 21, 22, 22, 23, 24, 24, 25, 26, 26, 27), (28, 29, 30), (34, 34, 34))
-CROSS_B_V = (10, 11, 13, 14)
+QUADS = ((0, 0), (0, 1), (1, 0), (1, 1), (2, 0), (2, 1))
+LOADS = (("wa", 0, 0), ("x", 0), ("x", 1), ("wa", 1, 0), ("x", 2), ("x", 3), ("wb", 0, 0), ("wb", 1, 0), ("wa", 0, 1), ("wb", 0, 1), ("wa", 1, 1), ("wb", 1, 1),
+    ("x", 4), ("x", 5), ("ub", 0, 0), ("ub", 1, 0), ("ua", 0, 0), ("ua", 1, 0), ("ua", 0, 1), ("ua", 1, 1), ("x", 6), ("x", 7))
+HB, VLAG, SLAG, HLAG, TLAG = 4, 2, 1, 1, 1
+QLAG = 2
+ZA = (4,4,4,0,4,2)
+ZB = (4,4,0,4,0,2)
+WR = (4,4,4,4,0,4,0,4,0,4)
+WS = (0,0,1,2,2,4,4,6,6,7)
+SCHED = tuple((WS[n], key, WR[n]) for n, key in enumerate((("wa", 0, 1), ("wb", 0, 1), ("wa", 1, 1), ("wb", 1, 1), ("ub", 0, 0), ("ub", 1, 0), ("ua", 0, 0), ("ua", 1, 0), ("ua", 0, 1), ("ua", 1, 1)))) + tuple((4 * q + 3 + VLAG, ("zb",) + QUADS[q], ZB[q]) for q in range(len(QUADS))) + tuple((4 * q + 3 + VLAG, ("za",) + QUADS[q], ZA[q]) for q in range(len(QUADS)))
+XSTEP = (2, 11)
+HEADSTEP = ((11,12,12,13,14,14,15,16,16,17,18,18),(20,20,21,21,22,23),(27,27,28,28,29,29))
+CROSS_B_V = ()

@@ -16,10 +16,25 @@ ACT = mybir.ActivationFunctionType
 ALU = mybir.AluOpType
 
 P = 128
-PACK = 4
-KP = P * PACK
+SLOTS = 4
+PASS = P * SLOTS
 BANK = 512
-CHUNKS = ((0, 512), (512, 256), (768, 256))
+PASSES = 2
+
+CHUNKS = ((0, 512), (512, 384), (896, 128))
+VECTOR_SLOTS = 3
+
+B_A, B_B, ST_AA, ST_AB, ST_BA, ST_BB = range(6)
+TASKS = {"a": (0, ST_AA, ST_AB), "b": (1, ST_BB, ST_BA)}
+
+
+def pieces(width):
+    out, lo = [], 0
+    for size in (512, 256, 128):
+        if width - lo >= size:
+            out.append(slice(lo, lo + size))
+            lo += size
+    return out
 
 
 def tile_cross_stitch_task_heads_f3_kernel(
@@ -30,312 +45,327 @@ def tile_cross_stitch_task_heads_f3_kernel(
         keep = ctx.enter_context(tc.tile_pool(name="keep", bufs=1))
         work = ctx.enter_context(tc.tile_pool(name="work", bufs=2))
         psum = ctx.enter_context(tc.psum_pool(name="psum", bufs=4))
-        ctx.enter_context(tc.manual_schedule())
 
         ident32 = keep.tile([P, P], F32, name="ident32")
         make_identity(nc, ident32[:])
         ident16 = keep.tile([P, P], BF16, name="ident16")
         make_identity(nc, ident16[:])
 
-        vec_rows = keep.tile([P, KP], BF16, name="vec_rows")
-        nc.vector.memset(vec_rows[:], 0.0)
-        for i, v in enumerate((b_a, b_b, st_aa, st_ab, st_ba, st_bb)):
-            nc.scalar.dma_start(out=vec_rows[2 * i : 2 * i + 2, :], in_=v.rearrange("(g c) -> g c", g=2))
-        vec = keep.tile([P, PACK, 12], F32, name="vec")
         warm = keep.tile([P, 1], F32, name="warm")
         nc.scalar.activation(out=warm[:], in_=ident32[:, 0:1], func=ACT.Silu)
 
-        def spread_vectors():
-            bank = psum.tile([P, PACK, P], BF16, name="bank")
-            for t in range(PACK):
-                nc.tensor.transpose(bank[:, t, :], vec_rows[:, t::PACK], ident16[:])
-            nc.scalar.copy(out=vec[:], in_=bank[:, :, 0:12])
+        small_rows = keep.tile([P, PASS], BF16, name="small_rows")
+        nc.vector.memset(small_rows[:], 0.0)
+        gains = keep.tile([P, SLOTS, 12], F32, name="gains")
+        head_bias = keep.tile([P, PA + RB], BF16, name="head_bias")
 
-        raw = {}
+        def load_small():
+            for i, v in enumerate((b_a, b_b, st_aa, st_ab, st_ba, st_bb, c_a, c_b)):
+                half = v.shape[0] // 2
+                nc.sync.dma_start(out=small_rows[2 * i : 2 * i + 2, 0:half], in_=v.rearrange("(g c) -> g c", g=2))
 
-        def load_block(key, src, kp, half):
-            t = keep.tile([P, PACK, BANK], BF16, name="raw_%s%d%d" % key)
-            rows = src[kp * KP : (kp + 1) * KP, half * BANK : (half + 1) * BANK]
-            nc.sync.dma_start(out=t[:], in_=rows.rearrange("(p j) c -> p j c", j=PACK))
-            raw[key] = t
+        def spread_gains():
+            bank = psum.tile([P, SLOTS, P], BF16, name="aux")
+            for t in range(SLOTS):
+                nc.tensor.transpose(bank[:, t, :], small_rows[:, t::SLOTS], ident16[:])
+            nc.scalar.copy(out=gains[:], in_=bank[:, :, 0:12])
 
-        def load_x(a):
-            t = keep.tile([P, K], BF16, name="x_raw%d" % a)
-            nc.sync.dma_start(out=t[:], in_=x[a * P : (a + 1) * P, :])
-            raw[("x", a)] = t
+        def gain(i, g, t):
+            return gains[:, t, 2 * i + g : 2 * i + g + 1]
 
-        srcs = {"wa": w_a, "wb": w_b, "ua": u_a, "ub": u_b}
-        for key in LOADS:
-            if key[0] == "x":
-                load_x(key[1])
-            else:
-                load_block(key, srcs[key[0]], key[1], key[2])
-        ca_all = keep.tile([P, PA], BF16, name="ca_all")
-        nc.sync.dma_start(out=ca_all[:], in_=c_a.partition_broadcast(P))
-        cb_all = keep.tile([P, RB], BF16, name="cb_all")
-        nc.sync.dma_start(out=cb_all[:], in_=c_b.partition_broadcast(P))
+        def spread_head_bias():
+            for row, first, half in ((12, 0, PA // 2), (14, PA, RB // 2)):
+                bank = psum.tile([P, 2 * half], BF16, name="aux")
+                for r in range(2):
+                    nc.tensor.matmul(
+                        out=bank[:, r * half : (r + 1) * half],
+                        lhsT=ident16[:, row + r : row + r + 1].to_broadcast([P, P]),
+                        rhs=small_rows[:, 0:half],
+                        start=True,
+                        stop=True,
+                    )
+                nc.scalar.copy(out=head_bias[:, first : first + 2 * half], in_=bank[:])
 
-        grouped = {}
+        weights = {"wa": w_a, "wb": w_b, "ua": u_a, "ub": u_b}
+        rows_of = {}
+        regrouped = {}
         codes = {}
         scales = {}
 
-        def group_direct(key, src, width, permute, shared):
-            t = work.tile([P, PACK * width], BF16, name="grouped", bufs=5, align_bytes=64)
-            if permute:
-                dst = t[:].rearrange("p (t c i j) -> p c j i t", t=PACK, i=2, j=PACK)
-                rows = src[:].rearrange("p j (c i t) -> p c j i t", i=2, t=PACK)
-                if shared > 0:
-                    nc.vector.tensor_copy(out=dst[:, :, :, :, 0:shared], in_=rows[:, :, :, :, 0:shared])
-                if shared < PACK:
-                    nc.scalar.copy(out=dst[:, :, :, :, shared:], in_=rows[:, :, :, :, shared:])
-            else:
-                dst = t[:].rearrange("p (c i j) -> p c j i", i=4, j=PACK)
-                rows = src[:].rearrange("p j (c i) -> p c j i", i=4)
-                cut = shared * width // 16
-                if cut > 0:
-                    nc.vector.tensor_copy(out=dst[:, 0:cut], in_=rows[:, 0:cut])
-                if shared < PACK:
-                    nc.scalar.copy(out=dst[:, cut:], in_=rows[:, cut:])
-            grouped[key] = t
+        def load_block(key):
+            name, kp, half = key
+            raw = work.tile([P, SLOTS, BANK], BF16, name="raw", bufs=10)
+            block = weights[name][kp * PASS : (kp + 1) * PASS, half * BANK : (half + 1) * BANK]
+            nc.sync.dma_start(out=raw[:], in_=block.rearrange("(p j) c -> p j c", j=SLOTS))
+            rows_of[key] = raw[:]
 
-        def quantize_block(key):
-            c = keep.tile([P, BANK], U32, name="codes_%s%d%d" % key, align_bytes=64)
-            s = keep.tile([P, BANK], U8, name="scales_%s%d%d" % key, align_bytes=64)
-            nc.vector.quantize_mx(out=c[:].bitcast(E4M3), scales=s[:], in_=grouped.pop(key)[:])
-            codes[key], scales[key] = c, s
+        def load_block_pair(name, kp):
+            raw = work.tile([P, SLOTS, 2 * BANK], BF16, name="raw_pair")
+            block = weights[name][kp * PASS : (kp + 1) * PASS, :]
+            nc.sync.dma_start(out=raw[:], in_=block.rearrange("(p j) c -> p j c", j=SLOTS))
+            for half in range(2):
+                rows_of[(name, kp, half)] = raw[:, :, half * BANK : (half + 1) * BANK]
 
-        xt = {}
+        def new_regrouped(key, width):
+            regrouped[key] = work.tile([P, SLOTS * width], BF16, name="regrouped", bufs=4, align_bytes=64)
+            return regrouped[key]
 
-        xbank = {}
+        def regroup_dealt(key, vector_slots):
+            dst = new_regrouped(key, BANK)[:].rearrange("p (t c i j) -> p c j i t", t=SLOTS, i=2, j=SLOTS)
+            src = rows_of.pop(key).rearrange("p j (c i t) -> p c j i t", i=2, t=SLOTS)
+            nc.vector.tensor_copy(out=dst[:, :, :, :, 0:vector_slots], in_=src[:, :, :, :, 0:vector_slots])
+            if vector_slots < SLOTS:
+                nc.scalar.copy(out=dst[:, :, :, :, vector_slots:], in_=src[:, :, :, :, vector_slots:])
 
-        def transpose_x(ci, a):
-            t0, width = CHUNKS[ci]
-            words = raw[("x", t0 // P + a)][:].bitcast(F32)
-            bank = psum.tile([P, 2, 2, P], F32, name="bank")
-            for kp in range(2):
+        def regroup(key, copy):
+            src = rows_of.pop(key)
+            dst = new_regrouped(key, src.shape[2])
+            copy(
+                out=dst[:].rearrange("p (c i j) -> p c j i", i=4, j=SLOTS),
+                in_=src.rearrange("p j (c i) -> p c j i", i=4),
+            )
+
+        def quantize(key, fmt):
+            src = regrouped.pop(key)
+            width = src.shape[1] // SLOTS
+            codes[key] = keep.tile([P, width], U32, name="codes_%s%d%d" % key, align_bytes=64)
+            scales[key] = keep.tile([P, width], U8, name="scales_%s%d%d" % key, align_bytes=64)
+            for cols in pieces(width):
+                nc.vector.quantize_mx(
+                    out=codes[key][:, cols].bitcast(fmt),
+                    scales=scales[key][:, cols],
+                    in_=src[:, SLOTS * cols.start : SLOTS * cols.stop],
+                )
+
+        x_raw = {}
+        x_words = {}
+
+        def load_x(a):
+            x_raw[a] = keep.tile([P, K], BF16, name="x_raw%d" % a)
+            nc.sync.dma_start(out=x_raw[a][:], in_=x[a * P : (a + 1) * P, :])
+
+        def transpose_x(a):
+            half, pos = divmod(a, 4)
+            if pos == 0:
+                x_words[half] = work.tile([P, PASSES, BANK, 2], F32, name="x_words", bufs=1, align_bytes=64)
+            words = x_raw[a][:].bitcast(F32)
+            bank = psum.tile([P, PASSES, 2, P], F32, name="aux")
+            for kp in range(PASSES):
                 for u in range(2):
                     nc.tensor.transpose(bank[:, kp, u, :], words[:, 256 * kp + u : 256 * (kp + 1) : 2], ident32[:])
-            xbank[(ci, a)] = bank
-
-        def unstage_x(ci, a):
-            width = CHUNKS[ci][1]
-            if ci not in xt:
-                xt[ci] = work.tile([P, 2, width, 2], F32, name="xt%d" % width, bufs=1, align_bytes=64)
             nc.scalar.copy(
-                out=xt[ci][:, :, a * P : (a + 1) * P, :], in_=xbank.pop((ci, a))[:].rearrange("p k u r -> p k r u")
+                out=x_words[half][:, :, pos * P : (pos + 1) * P, :], in_=bank[:].rearrange("p k u r -> p k r u")
             )
 
-        def quantize_x(ci):
-            width = CHUNKS[ci][1]
-            c = keep.tile([P, 2 * width], U32, name="codes_x%d" % ci, align_bytes=64)
-            s = keep.tile([P, 2 * width], U8, name="scales_x%d" % ci, align_bytes=64)
+        def quantize_x(half):
+            key = ("x", half)
+            codes[key] = keep.tile([P, PASSES * BANK], U32, name="codes_x%d" % half, align_bytes=64)
+            scales[key] = keep.tile([P, PASSES * BANK], U8, name="scales_x%d" % half, align_bytes=64)
             nc.vector.quantize_mx(
-                out=c[:].bitcast(E4M3), scales=s[:], in_=xt[ci][:].rearrange("p k r u -> p (k r u)").bitcast(BF16)
+                out=codes[key][:].bitcast(E4M3),
+                scales=scales[key][:],
+                in_=x_words[half][:].rearrange("p k r u -> p (k r u)").bitcast(BF16),
             )
-            codes[("x", ci)], scales[("x", ci)] = c, s
 
-        units = [(ci, g, t) for ci, g in QUADS for t in range(PACK)]
-        pre = {}
+        units = [(ci, g, t) for ci in range(len(CHUNKS)) for g in range(PASSES) for t in range(SLOTS)]
+        sums = {}
         hidden = {}
-        zrows = {}
+        cross = {}
+        diagonal = {}
+        stitched = {}
 
-        def branch_matmul(unit, nm):
+        def branch_matmul(unit, branch):
             ci, g, t = unit
+            half, first = divmod(CHUNKS[ci][0], BANK)
             width = CHUNKS[ci][1]
             bank = psum.tile([P, width], F32, name="pre")
-            for kp in range(2):
-                key = (nm, kp, g)
-                nc.tensor.matmul_mx(
-                    out=bank[:],
-                    lhsT=codes[key][:, t * P : (t + 1) * P].bitcast(E4M3),
-                    lhsT_scale=scales[key][:, t * P : (t + 1) * P],
-                    rhs=codes[("x", ci)][:, kp * width : (kp + 1) * width].bitcast(E4M3),
-                    rhs_scale=scales[("x", ci)][:, kp * width : (kp + 1) * width],
-                    start=(kp == 0),
-                    stop=(kp == 1),
-                )
-            pre[(unit, nm)] = bank
-
-        def column(i, unit):
-            j = 2 * i + unit[1]
-            return vec[:, unit[2], j : j + 1]
+            for cols in pieces(width):
+                for kp in range(PASSES):
+                    key = (("wa", "wb")[branch], kp, g)
+                    tokens = slice(kp * BANK + first + cols.start, kp * BANK + first + cols.stop)
+                    nc.tensor.matmul_mx(
+                        out=bank[:, cols],
+                        lhsT=codes[key][:, t * P : (t + 1) * P].bitcast(E4M3),
+                        lhsT_scale=scales[key][:, t * P : (t + 1) * P],
+                        rhs=codes[("x", half)][:, tokens].bitcast(E4M3),
+                        rhs_scale=scales[("x", half)][:, tokens],
+                        start=(kp == 0),
+                        stop=(kp == PASSES - 1),
+                    )
+            sums[(unit, branch)] = bank
 
         def activate(unit):
-            width = CHUNKS[unit[0]][1]
-            h_a = work.tile([P, width], F32, name="h_a", bufs=HB)
-            h_b = work.tile([P, width], F32, name="h_b", bufs=HB)
-            nc.scalar.activation(out=h_a[:], in_=pre.pop((unit, "wa"))[:], func=ACT.Silu, bias=column(0, unit))
-            nc.scalar.activation(out=h_b[:], in_=pre.pop((unit, "wb"))[:], func=ACT.Silu, bias=column(1, unit))
-            hidden[unit] = (h_a, h_b)
+            ci, g, t = unit
+            for branch in range(2):
+                h = work.tile([P, CHUNKS[ci][1]], F32, name="h%d" % branch, bufs=5)
+                nc.scalar.activation(
+                    out=h[:], in_=sums.pop((unit, branch))[:], func=ACT.Silu, bias=gain((B_A, B_B)[branch], g, t)
+                )
+                hidden[(unit, branch)] = h
+
+        def elementwise_tasks(unit):
+            return ("a",) if unit[0] == 0 else ("b", "a")
 
         def cross_terms(unit):
-            width = CHUNKS[unit[0]][1]
-            h_a, h_b = hidden[unit]
-            cross_a = work.tile([P, width], F32, name="cross_a", bufs=HB - 1)
-            cross_b = work.tile([P, width], F32, name="cross_b", bufs=HB - 1)
-            if units.index(unit) in CROSS_B_V:
-                nc.vector.tensor_scalar(out=cross_b[:], in0=h_a[:], scalar1=column(4, unit), scalar2=None, op0=ALU.mult)
-            else:
-                nc.scalar.activation(out=cross_b[:], in_=h_a[:], func=ACT.Copy, scale=column(4, unit))
-            nc.scalar.activation(out=cross_a[:], in_=h_b[:], func=ACT.Copy, scale=column(3, unit))
-            hidden[unit] = (h_a, h_b, cross_a, cross_b)
+            ci, g, t = unit
+            for task in elementwise_tasks(unit):
+                own, own_gain, other_gain = TASKS[task]
+                term = work.tile([P, CHUNKS[ci][1]], F32, name="cross_" + task, bufs=3)
+                nc.scalar.activation(
+                    out=term[:], in_=hidden[(unit, 1 - own)][:], func=ACT.Copy, scale=gain(other_gain, g, t)
+                )
+                cross[(task, unit)] = term
 
         def stitch(unit):
             ci, g, t = unit
-            width = CHUNKS[ci][1]
-            h_a, h_b, cross_a, cross_b = hidden.pop(unit)
+            for task in elementwise_tasks(unit):
+                own, own_gain, other_gain = TASKS[task]
+                key = ("z" + task, ci, g)
+                if t == 0:
+                    rows_of[key] = work.tile([P, SLOTS, CHUNKS[ci][1]], BF16, name="z_rows_" + task)[:]
+                nc.vector.scalar_tensor_tensor(
+                    out=rows_of[key][:, t, :],
+                    in0=hidden[(unit, own)][:],
+                    scalar=gain(own_gain, g, t),
+                    in1=cross.pop((task, unit))[:],
+                    op0=ALU.mult,
+                    op1=ALU.add,
+                )
+
+        def make_diagonals(g):
+            for t in range(SLOTS):
+                for i in (ST_BA, ST_BB):
+                    diagonal[(i, g, t)] = keep.tile([P, P], F32, name="diagonal%d%d%d" % (i, g, t))
+                    nc.vector.tensor_scalar(
+                        out=diagonal[(i, g, t)][:], in0=ident32[:], scalar1=gain(i, g, t), scalar2=None, op0=ALU.mult
+                    )
+
+        def stitch_on_tensor(unit):
+            ci, g, t = unit
             if t == 0:
-                zrows[("zb", ci, g)] = work.tile([P, PACK, width], BF16, name="zrows_b")
-                zrows[("za", ci, g)] = work.tile([P, PACK, width], BF16, name="zrows_a")
-            nc.vector.scalar_tensor_tensor(
-                out=zrows[("zb", ci, g)][:, t, :], in0=h_b[:], scalar=column(5, unit), in1=cross_b[:], op0=ALU.mult, op1=ALU.add
-            )
-            nc.vector.scalar_tensor_tensor(
-                out=zrows[("za", ci, g)][:, t, :], in0=h_a[:], scalar=column(2, unit), in1=cross_a[:], op0=ALU.mult, op1=ALU.add
-            )
+                stitched[g] = [psum.tile([P, SLOTS, P], F32, name="aux") for a in range(CHUNKS[ci][1] // P)]
+            for a, bank in enumerate(stitched[g]):
+                for branch, i in enumerate((ST_BA, ST_BB)):
+                    nc.tensor.matmul(
+                        out=bank[:, t, :],
+                        lhsT=diagonal[(i, g, t)][:],
+                        rhs=hidden[(unit, branch)][:, a * P : (a + 1) * P],
+                        start=(branch == 0),
+                        stop=(branch == 1),
+                    )
 
-        def quantize_z(key):
-            width = CHUNKS[key[1]][1]
-            c = keep.tile([P, width], U32, name="codes_%s%d%d" % key, align_bytes=64)
-            s = keep.tile([P, width], U8, name="scales_%s%d%d" % key, align_bytes=64)
-            nc.vector.quantize_mx(out=c[:].bitcast(E5M2), scales=s[:], in_=grouped.pop(key)[:])
-            codes[key], scales[key] = c, s
+        def finish_z(ci, g):
+            key_a, key_b = ("za", ci, g), ("zb", ci, g)
+            if ci == 0:
+                dst = new_regrouped(key_b, CHUNKS[ci][1])
+                for a, bank in enumerate(stitched.pop(g)):
+                    nc.scalar.copy(
+                        out=dst[:, a * BANK : (a + 1) * BANK].rearrange("p (n t) -> p n t", t=SLOTS),
+                        in_=bank[:].rearrange("p t n -> p n t"),
+                    )
+            else:
+                regroup(key_b, nc.scalar.copy)
+            regroup(key_a, nc.vector.tensor_copy)
 
-        heads = {}
-        y_rows = {}
+        def quantize_z(ci, g):
+            quantize(("zb", ci, g), E5M2)
+            quantize(("za", ci, g), E5M2)
 
-        def head_matmul(ci, a, nm, half):
-            bank = psum.tile([P, BANK], F32, name="bank")
-            for g in range(2):
-                zkey, ukey = ("z" + nm, ci, g), ("u" + nm, g, half)
+        def head(ci, a, task, half):
+            bank = psum.tile([P, BANK], F32, name="aux")
+            for g in range(PASSES):
+                z_key, u_key = ("z" + task, ci, g), ("u" + task, g, half)
                 nc.tensor.matmul_mx(
                     out=bank[:],
-                    lhsT=codes[zkey][:, a * P : (a + 1) * P].bitcast(E5M2),
-                    lhsT_scale=scales[zkey][:, a * P : (a + 1) * P],
-                    rhs=codes[ukey][:].bitcast(E4M3),
-                    rhs_scale=scales[ukey][:],
+                    lhsT=codes[z_key][:, a * P : (a + 1) * P].bitcast(E5M2),
+                    lhsT_scale=scales[z_key][:, a * P : (a + 1) * P],
+                    rhs=codes[u_key][:].bitcast(E4M3),
+                    rhs_scale=scales[u_key][:],
                     start=(g == 0),
-                    stop=(g == 1),
+                    stop=(g == PASSES - 1),
                 )
-            heads[(ci, a, nm, half)] = bank
-
-        def head_finish(ci, a, nm, half):
-            bank = heads.pop((ci, a, nm, half))
-            rows = slice(CHUNKS[ci][0] + a * P, CHUNKS[ci][0] + (a + 1) * P)
-            cols = slice(half * BANK, (half + 1) * BANK)
-            if nm == "a":
+            tokens = slice(CHUNKS[ci][0] + a * P, CHUNKS[ci][0] + (a + 1) * P)
+            if task == "a":
+                cols = slice(half * BANK, (half + 1) * BANK)
                 y = work.tile([P, BANK], F32, name="y_a", bufs=4)
-                nc.vector.tensor_tensor(out=y[:], in0=bank[:], in1=ca_all[:, cols], op=ALU.add)
-                nc.sync.dma_start(out=out_0[rows, cols], in_=y[:])
+                nc.vector.tensor_tensor(out=y[:], in0=bank[:], in1=head_bias[:, cols], op=ALU.add)
+                nc.sync.dma_start(out=out_0[tokens, cols], in_=y[:])
             else:
-                y = work.tile([P, BANK], F32, name="y_b", bufs=3)
-                nc.vector.tensor_tensor(out=y[:], in0=bank[:], in1=cb_all[:], op=ALU.add)
-                y_rows[(ci, a, "b")] = y
+                logits = work.tile([P, BANK], F32, name="logits_b", bufs=3)
+                nc.vector.tensor_tensor(out=logits[:], in0=bank[:], in1=head_bias[:, PA:], op=ALU.add)
+                y = work.tile([P, BANK], F32, name="y_b")
+                nc.scalar.activation(out=y[:], in_=logits[:], func=ACT.Tanh)
+                nc.sync.dma_start(out=out_1[tokens, :], in_=y[:])
 
-        def head_tanh(ci, a):
-            rows = slice(CHUNKS[ci][0] + a * P, CHUNKS[ci][0] + (a + 1) * P)
-            yt = work.tile([P, BANK], F32, name="y_tanh", bufs=2)
-            nc.scalar.activation(out=yt[:], in_=y_rows.pop((ci, a, "b"))[:], func=ACT.Tanh)
-            nc.sync.dma_start(out=out_1[rows, :], in_=yt[:])
+        load_block(("wa", 0, 0))
+        load_x(0)
+        load_small()
+        load_x(1)
+        load_block(("wa", 1, 0))
+        load_x(2)
+        load_x(3)
+        for kp in range(PASSES):
+            load_block(("wb", kp, 0))
+        for a in range(4, 8):
+            load_x(a)
+        second_channels = [(name, kp, 1) for kp in range(PASSES) for name in ("wa", "wb")]
+        for key in second_channels:
+            load_block(key)
+        for g in range(PASSES):
+            load_block(("ub", g, 0))
+        for g in range(PASSES):
+            load_block_pair("ua", g)
 
-        def group(key, route):
-            src = zrows.pop(key) if key[0][0] == "z" else raw[key]
-            if True:
-                group_direct(key, src, width_of(key), key[0][0] == "w", PACK if route == "V" else route)
-
-        def quant(key):
-            if key[0][0] == "z":
-                quantize_z(key)
-            else:
-                quantize_block(key)
-
-        def width_of(key):
-            return CHUNKS[key[1]][1] if key[0][0] == "z" else BANK
-
-        group(("wa", 0, 0), 3)
-        spread_vectors()
-        for a in range(CHUNKS[0][1] // P):
-            transpose_x(0, a)
-            unstage_x(0, a)
-            if a == 0:
-                quant(("wa", 0, 0))
-            if a == 1:
-                group(("wa", 1, 0), 3)
-        quant(("wa", 1, 0))
+        for kp in range(PASSES):
+            regroup_dealt(("wa", kp, 0), VECTOR_SLOTS)
+            transpose_x(2 * kp)
+            transpose_x(2 * kp + 1)
+            quantize(("wa", kp, 0), E4M3)
+        spread_gains()
         quantize_x(0)
-        branch_matmul(units[0], "wa")
-        group(("wb", 0, 0), 2)
-        quant(("wb", 0, 0))
-        group(("wb", 1, 0), 2)
-        quant(("wb", 1, 0))
-        branch_matmul(units[0], "wb")
+        branch_matmul(units[0], 0)
+        for kp in range(PASSES):
+            regroup_dealt(("wb", kp, 0), VECTOR_SLOTS)
+            quantize(("wb", kp, 0), E4M3)
+        branch_matmul(units[0], 1)
+        make_diagonals(0)
+        spread_head_bias()
 
-        steps = len(units) + 12
-        on_tensor = [[] for u in range(steps)]
-        on_scalar = [[] for u in range(steps)]
-        early = [[] for u in range(steps)]
-        late = [[] for u in range(steps)]
-
-        def plan_block(step, key, route):
-            if route == 0:
-                on_scalar[step + SLAG].append(lambda: group(key, route))
-                late[step + SLAG + QLAG].append(lambda: quant(key))
+        steps = len(units) + 4
+        beside = [[] for step in range(steps)]
+        for a in range(4, 8):
+            beside[(a - 4) // 2].append(lambda a=a: transpose_x(a))
+        beside[2].append(lambda: make_diagonals(1))
+        beside[3].append(lambda: quantize_x(1))
+        head_blocks = [("ub", g, 0) for g in range(PASSES)] + [("ua", g, h) for g in range(PASSES) for h in range(2)]
+        for step, key in enumerate(second_channels + head_blocks):
+            if key[0] in ("wa", "wb"):
+                beside[step].append(lambda key=key: regroup_dealt(key, SLOTS))
             else:
-                late[step].append(lambda: group(key, route))
-                late[step + 1].append(lambda: quant(key))
-
-        def plan_head(step, args):
-            on_tensor[step].append(lambda: head_matmul(*args))
-            late[step + HLAG].append(lambda: head_finish(*args))
-            if args[2] == "b":
-                on_scalar[step + HLAG + TLAG].append(lambda: head_tanh(args[0], args[1]))
-
-        def plan_x(step, ci):
-            tiles = CHUNKS[ci][1] // P
-            for a in range(tiles):
-                on_tensor[step + a].append(lambda a=a: transpose_x(ci, a))
-                on_scalar[step + a + 1].append(lambda a=a: unstage_x(ci, a))
-            late[step + tiles + 1].append(lambda: quantize_x(ci))
-
-        for s, key, route in SCHED:
-            plan_block(s, key, route)
-        for ci in range(1, len(CHUNKS)):
-            plan_x(XSTEP[ci - 1], ci)
+                copy = nc.scalar.copy if key[0] == "ub" else nc.vector.tensor_copy
+                beside[step].append(lambda key=key, copy=copy: regroup(key, copy))
+            beside[step].append(lambda key=key: quantize(key, E4M3))
         for ci in range(len(CHUNKS)):
-            jobs = [(ci, a + da, nm, half) for a in range(0, CHUNKS[ci][1] // P, 2) for da, nm, half in ((0, "b", 0), (1, "b", 0), (0, "a", 0), (0, "a", 1), (1, "a", 0), (1, "a", 1))]
-            for n, args in enumerate(jobs):
-                plan_head(HEADSTEP[ci][n], args)
+            last = [PASSES * SLOTS * ci + SLOTS * g + SLOTS - 1 for g in range(PASSES)]
+            for g in range(PASSES):
+                beside[last[g] + 2].append(lambda ci=ci, g=g: finish_z(ci, g))
+                beside[last[g] + 3].append(lambda ci=ci, g=g: quantize_z(ci, g))
+            jobs = [(ci, a, task, half) for a in range(CHUNKS[ci][1] // P) for task, half in (("b", 0), ("a", 0), ("a", 1))]
+            span = min(PASSES * SLOTS, steps - last[1] - 4)
+            for n, job in enumerate(jobs):
+                beside[last[1] + 4 + n * span // len(jobs)].append(lambda job=job: head(*job))
 
         for i in range(steps):
             if i < len(units):
                 activate(units[i])
             if 1 <= i <= len(units):
                 cross_terms(units[i - 1])
-            for fn in on_scalar[i]:
-                fn()
-            for fn in early[i]:
-                fn()
-            if VLAG <= i < len(units) + VLAG:
-                stitch(units[i - VLAG])
-            for fn in late[i]:
-                fn()
+            if 2 <= i <= len(units) + 1:
+                stitch(units[i - 2])
+            for job in beside[i]:
+                job()
             if i + 1 < len(units):
-                branch_matmul(units[i + 1], "wa")
-                branch_matmul(units[i + 1], "wb")
-            for fn in on_tensor[i]:
-                fn()
-
-
-QUADS = ((0, 0), (0, 1), (1, 0), (1, 1), (2, 0), (2, 1))
-LOADS = (("wa", 0, 0), ("x", 0), ("x", 1), ("wa", 1, 0), ("x", 2), ("x", 3), ("wb", 0, 0), ("wb", 1, 0), ("wa", 0, 1), ("wb", 0, 1), ("wa", 1, 1), ("wb", 1, 1),
-    ("x", 4), ("x", 5), ("ub", 0, 0), ("ub", 1, 0), ("ua", 0, 0), ("ua", 1, 0), ("ua", 0, 1), ("ua", 1, 1), ("x", 6), ("x", 7))
-HB, VLAG, SLAG, HLAG, TLAG = 4, 2, 1, 1, 1
-QLAG = 2
-ZA = (4,4,4,0,4,2)
-ZB = (4,4,0,4,0,2)
-WR = (4,4,4,4,0,4,0,4,0,4)
-WS = (0,0,1,2,2,4,4,6,6,7)
-SCHED = tuple((WS[n], key, WR[n]) for n, key in enumerate((("wa", 0, 1), ("wb", 0, 1), ("wa", 1, 1), ("wb", 1, 1), ("ub", 0, 0), ("ub", 1, 0), ("ua", 0, 0), ("ua", 1, 0), ("ua", 0, 1), ("ua", 1, 1)))) + tuple((4 * q + 3 + VLAG, ("zb",) + QUADS[q], ZB[q]) for q in range(len(QUADS))) + tuple((4 * q + 3 + VLAG, ("za",) + QUADS[q], ZA[q]) for q in range(len(QUADS)))
-XSTEP = (2, 11)
-HEADSTEP = ((11,12,12,13,14,14,15,16,16,17,18,18),(20,20,21,21,22,23),(27,27,28,28,29,29))
-CROSS_B_V = ()
+                branch_matmul(units[i + 1], 0)
+                branch_matmul(units[i + 1], 1)
+            if 1 <= i <= PASSES * SLOTS:
+                stitch_on_tensor(units[i - 1])

@@ -24,6 +24,8 @@ PASSES = 2
 CHUNKS = ((0, 512), (512, 384), (896, 128))
 VECTOR_SLOTS = 3
 
+ON_TENSOR = ((0, 1), (2, 1))
+
 B_A, B_B, ST_AA, ST_AB, ST_BA, ST_BB = range(6)
 TASKS = {"a": (0, ST_AA, ST_AB), "b": (1, ST_BB, ST_BA)}
 
@@ -57,12 +59,10 @@ def tile_cross_stitch_task_heads_f3_kernel(
         small_rows = keep.tile([P, PASS], BF16, name="small_rows")
         nc.vector.memset(small_rows[:], 0.0)
         gains = keep.tile([P, SLOTS, 12], F32, name="gains")
-        head_bias = keep.tile([P, PA + RB], BF16, name="head_bias")
 
         def load_small():
-            for i, v in enumerate((b_a, b_b, st_aa, st_ab, st_ba, st_bb, c_a, c_b)):
-                half = v.shape[0] // 2
-                nc.sync.dma_start(out=small_rows[2 * i : 2 * i + 2, 0:half], in_=v.rearrange("(g c) -> g c", g=2))
+            for i, v in enumerate((b_a, b_b, st_aa, st_ab, st_ba, st_bb)):
+                nc.sync.dma_start(out=small_rows[2 * i : 2 * i + 2, :], in_=v.rearrange("(g c) -> g c", g=PASSES))
 
         def spread_gains():
             bank = psum.tile([P, SLOTS, P], BF16, name="aux")
@@ -72,19 +72,6 @@ def tile_cross_stitch_task_heads_f3_kernel(
 
         def gain(i, g, t):
             return gains[:, t, 2 * i + g : 2 * i + g + 1]
-
-        def spread_head_bias():
-            for row, first, half in ((12, 0, PA // 2), (14, PA, RB // 2)):
-                bank = psum.tile([P, 2 * half], BF16, name="aux")
-                for r in range(2):
-                    nc.tensor.matmul(
-                        out=bank[:, r * half : (r + 1) * half],
-                        lhsT=ident16[:, row + r : row + r + 1].to_broadcast([P, P]),
-                        rhs=small_rows[:, 0:half],
-                        start=True,
-                        stop=True,
-                    )
-                nc.scalar.copy(out=head_bias[:, first : first + 2 * half], in_=bank[:])
 
         weights = {"wa": w_a, "wb": w_b, "ua": u_a, "ub": u_b}
         rows_of = {}
@@ -204,7 +191,7 @@ def tile_cross_stitch_task_heads_f3_kernel(
                 hidden[(unit, branch)] = h
 
         def elementwise_tasks(unit):
-            return ("a",) if unit[0] == 0 else ("b", "a")
+            return ("a",) if unit[:2] in ON_TENSOR else ("b", "a")
 
         def cross_terms(unit):
             ci, g, t = unit
@@ -232,12 +219,13 @@ def tile_cross_stitch_task_heads_f3_kernel(
                     op1=ALU.add,
                 )
 
-        def make_diagonals(g):
+        def make_diagonals():
+            g = PASSES - 1
             for t in range(SLOTS):
                 for i in (ST_BA, ST_BB):
                     diagonal[(i, g, t)] = keep.tile([P, P], F32, name="diagonal%d%d%d" % (i, g, t))
-                    nc.vector.tensor_scalar(
-                        out=diagonal[(i, g, t)][:], in0=ident32[:], scalar1=gain(i, g, t), scalar2=None, op0=ALU.mult
+                    nc.scalar.activation(
+                        out=diagonal[(i, g, t)][:], in_=ident32[:], func=ACT.Copy, scale=gain(i, g, t)
                     )
 
         def stitch_on_tensor(unit):
@@ -256,7 +244,7 @@ def tile_cross_stitch_task_heads_f3_kernel(
 
         def finish_z(ci, g):
             key_a, key_b = ("za", ci, g), ("zb", ci, g)
-            if ci == 0:
+            if (ci, g) in ON_TENSOR:
                 dst = new_regrouped(key_b, CHUNKS[ci][1])
                 for a, bank in enumerate(stitched.pop(g)):
                     nc.scalar.copy(
@@ -288,11 +276,11 @@ def tile_cross_stitch_task_heads_f3_kernel(
             if task == "a":
                 cols = slice(half * BANK, (half + 1) * BANK)
                 y = work.tile([P, BANK], F32, name="y_a", bufs=4)
-                nc.vector.tensor_tensor(out=y[:], in0=bank[:], in1=head_bias[:, cols], op=ALU.add)
+                nc.vector.tensor_tensor(out=y[:], in0=bank[:], in1=bias_a[:, cols], op=ALU.add)
                 nc.sync.dma_start(out=out_0[tokens, cols], in_=y[:])
             else:
                 logits = work.tile([P, BANK], F32, name="logits_b", bufs=3)
-                nc.vector.tensor_tensor(out=logits[:], in0=bank[:], in1=head_bias[:, PA:], op=ALU.add)
+                nc.vector.tensor_tensor(out=logits[:], in0=bank[:], in1=bias_b[:], op=ALU.add)
                 y = work.tile([P, BANK], F32, name="y_b")
                 nc.scalar.activation(out=y[:], in_=logits[:], func=ACT.Tanh)
                 nc.sync.dma_start(out=out_1[tokens, :], in_=y[:])
@@ -302,10 +290,10 @@ def tile_cross_stitch_task_heads_f3_kernel(
         load_small()
         load_x(1)
         load_block(("wa", 1, 0))
+        load_block(("wb", 0, 0))
         load_x(2)
         load_x(3)
-        for kp in range(PASSES):
-            load_block(("wb", kp, 0))
+        load_block(("wb", 1, 0))
         for a in range(4, 8):
             load_x(a)
         second_channels = [(name, kp, 1) for kp in range(PASSES) for name in ("wa", "wb")]
@@ -315,27 +303,26 @@ def tile_cross_stitch_task_heads_f3_kernel(
             load_block(("ub", g, 0))
         for g in range(PASSES):
             load_block_pair("ua", g)
+        bias_a = keep.tile([P, PA], BF16, name="bias_a")
+        nc.sync.dma_start(out=bias_a[:], in_=c_a.partition_broadcast(P))
+        bias_b = keep.tile([P, RB], BF16, name="bias_b")
+        nc.sync.dma_start(out=bias_b[:], in_=c_b.partition_broadcast(P))
 
-        for kp in range(PASSES):
-            regroup_dealt(("wa", kp, 0), VECTOR_SLOTS)
-            transpose_x(2 * kp)
-            transpose_x(2 * kp + 1)
-            quantize(("wa", kp, 0), E4M3)
+        first_channels = [(name, kp, 0) for name in ("wa", "wb") for kp in range(PASSES)]
+        for a, key in enumerate(first_channels):
+            regroup_dealt(key, VECTOR_SLOTS)
+            transpose_x(a)
+            quantize(key, E4M3)
         spread_gains()
         quantize_x(0)
         branch_matmul(units[0], 0)
-        for kp in range(PASSES):
-            regroup_dealt(("wb", kp, 0), VECTOR_SLOTS)
-            quantize(("wb", kp, 0), E4M3)
         branch_matmul(units[0], 1)
-        make_diagonals(0)
-        spread_head_bias()
 
         steps = len(units) + 4
         beside = [[] for step in range(steps)]
         for a in range(4, 8):
             beside[(a - 4) // 2].append(lambda a=a: transpose_x(a))
-        beside[2].append(lambda: make_diagonals(1))
+        beside[2].append(make_diagonals)
         beside[3].append(lambda: quantize_x(1))
         head_blocks = [("ub", g, 0) for g in range(PASSES)] + [("ua", g, h) for g in range(PASSES) for h in range(2)]
         for step, key in enumerate(second_channels + head_blocks):
@@ -348,8 +335,8 @@ def tile_cross_stitch_task_heads_f3_kernel(
         for ci in range(len(CHUNKS)):
             last = [PASSES * SLOTS * ci + SLOTS * g + SLOTS - 1 for g in range(PASSES)]
             for g in range(PASSES):
-                beside[last[g] + 2].append(lambda ci=ci, g=g: finish_z(ci, g))
-                beside[last[g] + 3].append(lambda ci=ci, g=g: quantize_z(ci, g))
+                beside[last[g] + 2].insert(0, lambda ci=ci, g=g: finish_z(ci, g))
+                beside[last[g] + 3].insert(0, lambda ci=ci, g=g: quantize_z(ci, g))
             jobs = [(ci, a, task, half) for a in range(CHUNKS[ci][1] // P) for task, half in (("b", 0), ("a", 0), ("a", 1))]
             span = min(PASSES * SLOTS, steps - last[1] - 4)
             for n, job in enumerate(jobs):
@@ -367,5 +354,5 @@ def tile_cross_stitch_task_heads_f3_kernel(
             if i + 1 < len(units):
                 branch_matmul(units[i + 1], 0)
                 branch_matmul(units[i + 1], 1)
-            if 1 <= i <= PASSES * SLOTS:
+            if 1 <= i <= len(units) and units[i - 1][:2] in ON_TENSOR:
                 stitch_on_tensor(units[i - 1])

@@ -112,6 +112,21 @@ def tile_cross_stitch_task_heads_f3_kernel(
                 in_=src.rearrange("p j (c i) -> p c j i", i=4),
             )
 
+        def regroup_on_tensor(key):
+            src = rows_of.pop(key)
+            dst = new_regrouped(key, BANK)
+            for first in range(0, BANK, 256):
+                bank = psum.tile([P, SLOTS * 256], BF16, name="aux")
+                for j in range(0, SLOTS, 2):
+                    nc.tensor.matmul(
+                        out=bank[:].rearrange("p (c j) -> p c j", j=SLOTS)[:, :, j : j + 2],
+                        lhsT=ident16[:],
+                        rhs=src[:, j : j + 2, first : first + 256].rearrange("p j c -> p c j"),
+                        start=True,
+                        stop=True,
+                    )
+                nc.scalar.copy(out=dst[:, SLOTS * first : SLOTS * (first + 256)], in_=bank[:])
+
         def quantize(key, fmt):
             src = regrouped.pop(key)
             width = src.shape[1] // SLOTS
@@ -328,9 +343,10 @@ def tile_cross_stitch_task_heads_f3_kernel(
         for step, key in enumerate(second_channels + head_blocks):
             if key[0] in ("wa", "wb"):
                 beside[step].append(lambda key=key: regroup_dealt(key, SLOTS))
+            elif key[0] == "ub":
+                beside[step - 2].append(lambda key=key: regroup_on_tensor(key))
             else:
-                copy = nc.scalar.copy if key[0] == "ub" else nc.vector.tensor_copy
-                beside[step].append(lambda key=key, copy=copy: regroup(key, copy))
+                beside[step].append(lambda key=key: regroup(key, nc.vector.tensor_copy))
             beside[step].append(lambda key=key: quantize(key, E4M3))
         for ci in range(len(CHUNKS)):
             last = [PASSES * SLOTS * ci + SLOTS * g + SLOTS - 1 for g in range(PASSES)]

from contextlib import ExitStack

import concourse.mybir as mybir
from concourse.masks import make_identity

M, K, N, PA, RB = 1024, 1024, 1024, 1024, 512
FLOPS = 2 * M * K * 2 * N + 2 * M * N * (PA + RB)

F32 = mybir.dt.float32
BF16 = mybir.dt.bfloat16
U32 = mybir.dt.uint32
U8 = mybir.dt.uint8
E4M3 = mybir.dt.float8_e4m3fn_x4
E5M2 = mybir.dt.float8_e5m2_x4
ACT = mybir.ActivationFunctionType
ALU = mybir.AluOpType

P = 128
SLOTS = 4
PASS = P * SLOTS
BANK = 512
PASSES = 2

CHUNKS = ((0, 512), (512, 384), (896, 128))
VECTOR_SLOTS = 3

ON_TENSOR = ((0, 1), (2, 1))

B_A, B_B, ST_AA, ST_AB, ST_BA, ST_BB = range(6)
TASKS = {"a": (0, ST_AA, ST_AB), "b": (1, ST_BB, ST_BA)}


def pieces(width):
    out, lo = [], 0
    for size in (512, 256, 128):
        if width - lo >= size:
            out.append(slice(lo, lo + size))
            lo += size
    return out


def tile_cross_stitch_task_heads_f3_kernel(
    tc, x, w_a, w_b, b_a, b_b, st_aa, st_ab, st_ba, st_bb, u_a, u_b, c_a, c_b, out_0, out_1
):
    nc = tc.nc
    with ExitStack() as ctx:
        keep = ctx.enter_context(tc.tile_pool(name="keep", bufs=1))
        work = ctx.enter_context(tc.tile_pool(name="work", bufs=2))
        psum = ctx.enter_context(tc.psum_pool(name="psum", bufs=4))

        ident32 = keep.tile([P, P], F32, name="ident32")
        make_identity(nc, ident32[:])
        ident16 = keep.tile([P, P], BF16, name="ident16")
        make_identity(nc, ident16[:])

        warm = keep.tile([P, 1], F32, name="warm")
        nc.scalar.activation(out=warm[:], in_=ident32[:, 0:1], func=ACT.Silu)

        small_rows = keep.tile([P, PASS], BF16, name="small_rows")
        nc.vector.memset(small_rows[:], 0.0)
        gains = keep.tile([P, SLOTS, 12], F32, name="gains")

        def load_small():
            for i, v in enumerate((b_a, b_b, st_aa, st_ab, st_ba, st_bb)):
                nc.sync.dma_start(out=small_rows[2 * i : 2 * i + 2, :], in_=v.rearrange("(g c) -> g c", g=PASSES))

        def spread_gains():
            bank = psum.tile([P, SLOTS, P], BF16, name="aux")
            for t in range(SLOTS):
                nc.tensor.transpose(bank[:, t, :], small_rows[:, t::SLOTS], ident16[:])
            nc.scalar.copy(out=gains[:], in_=bank[:, :, 0:12])

        def gain(i, g, t):
            return gains[:, t, 2 * i + g : 2 * i + g + 1]

        weights = {"wa": w_a, "wb": w_b, "ua": u_a, "ub": u_b}
        rows_of = {}
        regrouped = {}
        codes = {}
        scales = {}

        def load_block(key):
            name, kp, half = key
            raw = work.tile([P, SLOTS, BANK], BF16, name="raw", bufs=10)
            block = weights[name][kp * PASS : (kp + 1) * PASS, half * BANK : (half + 1) * BANK]
            nc.sync.dma_start(out=raw[:], in_=block.rearrange("(p j) c -> p j c", j=SLOTS))
            rows_of[key] = raw[:]

        def load_block_pair(name, kp):
            raw = work.tile([P, SLOTS, 2 * BANK], BF16, name="raw_pair")
            block = weights[name][kp * PASS : (kp + 1) * PASS, :]
            nc.sync.dma_start(out=raw[:], in_=block.rearrange("(p j) c -> p j c", j=SLOTS))
            for half in range(2):
                rows_of[(name, kp, half)] = raw[:, :, half * BANK : (half + 1) * BANK]

        def new_regrouped(key, width):
            regrouped[key] = work.tile([P, SLOTS * width], BF16, name="regrouped", bufs=4, align_bytes=64)
            return regrouped[key]

        def regroup_dealt(key, vector_slots):
            dst = new_regrouped(key, BANK)[:].rearrange("p (t c i j) -> p c j i t", t=SLOTS, i=2, j=SLOTS)
            src = rows_of.pop(key).rearrange("p j (c i t) -> p c j i t", i=2, t=SLOTS)
            nc.vector.tensor_copy(out=dst[:, :, :, :, 0:vector_slots], in_=src[:, :, :, :, 0:vector_slots])
            if vector_slots < SLOTS:
                nc.scalar.copy(out=dst[:, :, :, :, vector_slots:], in_=src[:, :, :, :, vector_slots:])

        def regroup(key, copy):
            src = rows_of.pop(key)
            dst = new_regrouped(key, src.shape[2])
            copy(
                out=dst[:].rearrange("p (c i j) -> p c j i", i=4, j=SLOTS),
                in_=src.rearrange("p j (c i) -> p c j i", i=4),
            )

        def regroup_on_tensor(key):
            src = rows_of.pop(key)
            dst = new_regrouped(key, BANK)
            for first in range(0, BANK, 256):
                bank = psum.tile([P, SLOTS * 256], BF16, name="aux")
                for j in range(0, SLOTS, 2):
                    nc.tensor.matmul(
                        out=bank[:].rearrange("p (c j) -> p c j", j=SLOTS)[:, :, j : j + 2],
                        lhsT=ident16[:],
                        rhs=src[:, j : j + 2, first : first + 256].rearrange("p j c -> p c j"),
                        start=True,
                        stop=True,
                    )
                nc.scalar.copy(out=dst[:, SLOTS * first : SLOTS * (first + 256)], in_=bank[:])

        def quantize(key, fmt):
            src = regrouped.pop(key)
            width = src.shape[1] // SLOTS
            codes[key] = keep.tile([P, width], U32, name="codes_%s%d%d" % key, align_bytes=64)
            scales[key] = keep.tile([P, width], U8, name="scales_%s%d%d" % key, align_bytes=64)
            for cols in pieces(width):
                nc.vector.quantize_mx(
                    out=codes[key][:, cols].bitcast(fmt),
                    scales=scales[key][:, cols],
                    in_=src[:, SLOTS * cols.start : SLOTS * cols.stop],
                )

        x_raw = {}
        x_words = {}

        def load_x(a):
            x_raw[a] = keep.tile([P, K], BF16, name="x_raw%d" % a)
            nc.sync.dma_start(out=x_raw[a][:], in_=x[a * P : (a + 1) * P, :])

        def transpose_x(a):
            half, pos = divmod(a, 4)
            if pos == 0:
                x_words[half] = work.tile([P, PASSES, BANK, 2], F32, name="x_words", bufs=1, align_bytes=64)
            words = x_raw[a][:].bitcast(F32)
            bank = psum.tile([P, PASSES, 2, P], F32, name="aux")
            for kp in range(PASSES):
                for u in range(2):
                    nc.tensor.transpose(bank[:, kp, u, :], words[:, 256 * kp + u : 256 * (kp + 1) : 2], ident32[:])
            nc.scalar.copy(
                out=x_words[half][:, :, pos * P : (pos + 1) * P, :], in_=bank[:].rearrange("p k u r -> p k r u")
            )

        def quantize_x(half):
            key = ("x", half)
            codes[key] = keep.tile([P, PASSES * BANK], U32, name="codes_x%d" % half, align_bytes=64)
            scales[key] = keep.tile([P, PASSES * BANK], U8, name="scales_x%d" % half, align_bytes=64)
            nc.vector.quantize_mx(
                out=codes[key][:].bitcast(E4M3),
                scales=scales[key][:],
                in_=x_words[half][:].rearrange("p k r u -> p (k r u)").bitcast(BF16),
            )

        units = [(ci, g, t) for ci in range(len(CHUNKS)) for g in range(PASSES) for t in range(SLOTS)]
        sums = {}
        hidden = {}
        cross = {}
        diagonal = {}
        stitched = {}

        def branch_matmul(unit, branch):
            ci, g, t = unit
            half, first = divmod(CHUNKS[ci][0], BANK)
            width = CHUNKS[ci][1]
            bank = psum.tile([P, width], F32, name="pre")
            for cols in pieces(width):
                for kp in range(PASSES):
                    key = (("wa", "wb")[branch], kp, g)
                    tokens = slice(kp * BANK + first + cols.start, kp * BANK + first + cols.stop)
                    nc.tensor.matmul_mx(
                        out=bank[:, cols],
                        lhsT=codes[key][:, t * P : (t + 1) * P].bitcast(E4M3),
                        lhsT_scale=scales[key][:, t * P : (t + 1) * P],
                        rhs=codes[("x", half)][:, tokens].bitcast(E4M3),
                        rhs_scale=scales[("x", half)][:, tokens],
                        start=(kp == 0),
                        stop=(kp == PASSES - 1),
                    )
            sums[(unit, branch)] = bank

        def activate(unit):
            ci, g, t = unit
            for branch in range(2):
                h = work.tile([P, CHUNKS[ci][1]], F32, name="h%d" % branch, bufs=5)
                nc.scalar.activation(
                    out=h[:], in_=sums.pop((unit, branch))[:], func=ACT.Silu, bias=gain((B_A, B_B)[branch], g, t)
                )
                hidden[(unit, branch)] = h

        def elementwise_tasks(unit):
            return ("a",) if unit[:2] in ON_TENSOR else ("b", "a")

        def cross_terms(unit):
            ci, g, t = unit
            for task in elementwise_tasks(unit):
                own, own_gain, other_gain = TASKS[task]
                term = work.tile([P, CHUNKS[ci][1]], F32, name="cross_" + task, bufs=3)
                nc.scalar.activation(
                    out=term[:], in_=hidden[(unit, 1 - own)][:], func=ACT.Copy, scale=gain(other_gain, g, t)
                )
                cross[(task, unit)] = term

        def stitch(unit):
            ci, g, t = unit
            for task in elementwise_tasks(unit):
                own, own_gain, other_gain = TASKS[task]
                key = ("z" + task, ci, g)
                if t == 0:
                    rows_of[key] = work.tile([P, SLOTS, CHUNKS[ci][1]], BF16, name="z_rows_" + task)[:]
                nc.vector.scalar_tensor_tensor(
                    out=rows_of[key][:, t, :],
                    in0=hidden[(unit, own)][:],
                    scalar=gain(own_gain, g, t),
                    in1=cross.pop((task, unit))[:],
                    op0=ALU.mult,
                    op1=ALU.add,
                )

        def make_diagonals():
            g = PASSES - 1
            for t in range(SLOTS):
                for i in (ST_BA, ST_BB):
                    diagonal[(i, g, t)] = keep.tile([P, P], F32, name="diagonal%d%d%d" % (i, g, t))
                    nc.scalar.activation(
                        out=diagonal[(i, g, t)][:], in_=ident32[:], func=ACT.Copy, scale=gain(i, g, t)
                    )

        def stitch_on_tensor(unit):
            ci, g, t = unit
            if t == 0:
                stitched[g] = [psum.tile([P, SLOTS, P], F32, name="aux") for a in range(CHUNKS[ci][1] // P)]
            for a, bank in enumerate(stitched[g]):
                for branch, i in enumerate((ST_BA, ST_BB)):
                    nc.tensor.matmul(
                        out=bank[:, t, :],
                        lhsT=diagonal[(i, g, t)][:],
                        rhs=hidden[(unit, branch)][:, a * P : (a + 1) * P],
                        start=(branch == 0),
                        stop=(branch == 1),
                    )

        def finish_z(ci, g):
            key_a, key_b = ("za", ci, g), ("zb", ci, g)
            if (ci, g) in ON_TENSOR:
                dst = new_regrouped(key_b, CHUNKS[ci][1])
                for a, bank in enumerate(stitched.pop(g)):
                    nc.scalar.copy(
                        out=dst[:, a * BANK : (a + 1) * BANK].rearrange("p (n t) -> p n t", t=SLOTS),
                        in_=bank[:].rearrange("p t n -> p n t"),
                    )
            else:
                regroup(key_b, nc.scalar.copy)
            regroup(key_a, nc.vector.tensor_copy)

        def quantize_z(ci, g):
            quantize(("zb", ci, g), E5M2)
            quantize(("za", ci, g), E5M2)

        def head(ci, a, task, half):
            bank = psum.tile([P, BANK], F32, name="aux")
            for g in range(PASSES):
                z_key, u_key = ("z" + task, ci, g), ("u" + task, g, half)
                nc.tensor.matmul_mx(
                    out=bank[:],
                    lhsT=codes[z_key][:, a * P : (a + 1) * P].bitcast(E5M2),
                    lhsT_scale=scales[z_key][:, a * P : (a + 1) * P],
                    rhs=codes[u_key][:].bitcast(E4M3),
                    rhs_scale=scales[u_key][:],
                    start=(g == 0),
                    stop=(g == PASSES - 1),
                )
            tokens = slice(CHUNKS[ci][0] + a * P, CHUNKS[ci][0] + (a + 1) * P)
            if task == "a":
                cols = slice(half * BANK, (half + 1) * BANK)
                y = work.tile([P, BANK], F32, name="y_a", bufs=4)
                nc.vector.tensor_tensor(out=y[:], in0=bank[:], in1=bias_a[:, cols], op=ALU.add)
                nc.sync.dma_start(out=out_0[tokens, cols], in_=y[:])
            else:
                logits = work.tile([P, BANK], F32, name="logits_b", bufs=3)
                nc.vector.tensor_tensor(out=logits[:], in0=bank[:], in1=bias_b[:], op=ALU.add)
                y = work.tile([P, BANK], F32, name="y_b")
                nc.scalar.activation(out=y[:], in_=logits[:], func=ACT.Tanh)
                nc.sync.dma_start(out=out_1[tokens, :], in_=y[:])

        load_block(("wa", 0, 0))
        load_x(0)
        load_small()
        load_x(1)
        load_block(("wa", 1, 0))
        load_block(("wb", 0, 0))
        load_x(2)
        load_x(3)
        load_block(("wb", 1, 0))
        for a in range(4, 8):
            load_x(a)
        second_channels = [(name, kp, 1) for kp in range(PASSES) for name in ("wa", "wb")]
        for key in second_channels:
            load_block(key)
        for g in range(PASSES):
            load_block(("ub", g, 0))
        for g in range(PASSES):
            load_block_pair("ua", g)
        bias_a = keep.tile([P, PA], BF16, name="bias_a")
        nc.sync.dma_start(out=bias_a[:], in_=c_a.partition_broadcast(P))
        bias_b = keep.tile([P, RB], BF16, name="bias_b")
        nc.sync.dma_start(out=bias_b[:], in_=c_b.partition_broadcast(P))

        first_channels = [(name, kp, 0) for name in ("wa", "wb") for kp in range(PASSES)]
        for a, key in enumerate(first_channels):
            regroup_dealt(key, VECTOR_SLOTS)
            transpose_x(a)
            quantize(key, E4M3)
        spread_gains()
        quantize_x(0)
        branch_matmul(units[0], 0)
        branch_matmul(units[0], 1)

        steps = len(units) + 4
        beside = [[] for step in range(steps)]
        for a in range(4, 8):
            beside[(a - 4) // 2].append(lambda a=a: transpose_x(a))
        beside[2].append(make_diagonals)
        beside[3].append(lambda: quantize_x(1))
        head_blocks = [("ub", g, 0) for g in range(PASSES)] + [("ua", g, h) for g in range(PASSES) for h in range(2)]
        for step, key in enumerate(second_channels + head_blocks):
            if key[0] in ("wa", "wb"):
                beside[step].append(lambda key=key: regroup_dealt(key, SLOTS))
            elif key[0] == "ub":
                beside[step - 2].append(lambda key=key: regroup_on_tensor(key))
            else:
                beside[step].append(lambda key=key: regroup(key, nc.vector.tensor_copy))
            beside[step].append(lambda key=key: quantize(key, E4M3))
        for ci in range(len(CHUNKS)):
            last = [PASSES * SLOTS * ci + SLOTS * g + SLOTS - 1 for g in range(PASSES)]
            for g in range(PASSES):
                beside[last[g] + 2].insert(0, lambda ci=ci, g=g: finish_z(ci, g))
                beside[last[g] + 3].insert(0, lambda ci=ci, g=g: quantize_z(ci, g))
            jobs = [(ci, a, task, half) for a in range(CHUNKS[ci][1] // P) for task, half in (("b", 0), ("a", 0), ("a", 1))]
            span = min(PASSES * SLOTS, steps - last[1] - 4)
            for n, job in enumerate(jobs):
                beside[last[1] + 4 + n * span // len(jobs)].append(lambda job=job: head(*job))

        for i in range(steps):
            if i < len(units):
                activate(units[i])
            if 1 <= i <= len(units):
                cross_terms(units[i - 1])
            if 2 <= i <= len(units) + 1:
                stitch(units[i - 2])
            for job in beside[i]:
                job()
            if i + 1 < len(units):
                branch_matmul(units[i + 1], 0)
                branch_matmul(units[i + 1], 1)
            if 1 <= i <= len(units) and units[i - 1][:2] in ON_TENSOR:
                stitch_on_tensor(units[i - 1])
